import numpy as np
import ml_dtypes


def mxq(x, axis, fmt="e4m3"):
    dtype, down = {"e4m3": (ml_dtypes.float8_e4m3fn, 7), "e5m2": (ml_dtypes.float8_e5m2, 14)}[fmt]
    v = np.moveaxis(np.asarray(x, np.float32).astype(ml_dtypes.bfloat16).astype(np.float64), axis, -1)
    blocks = v.reshape(v.shape[:-1] + (-1, 32))
    amax = np.abs(blocks).max(-1, keepdims=True)
    byte = np.maximum(np.where(amax > 0, np.frexp(amax)[1] - 1 + 127, 0) - down, 1)
    scale = np.exp2(byte - 127.0)
    codes = (blocks / scale).astype(np.float32).astype(dtype).astype(np.float64)
    return np.moveaxis((codes * scale).reshape(v.shape), -1, axis)


WIDE = False


def mx_kscale(k):
    if not WIDE:
        return np.ones(k)
    levels = np.array([10, -10, 5, -5, 0])
    if k % 512:
        return np.exp2(np.random.permutation(np.resize(levels, k // 32))).repeat(32)
    a = np.empty((k // 512, 16))
    for p in range(k // 512):
        a[p, :8] = np.random.permutation(np.resize(levels, 8))
        for g in range(8):
            far = levels[np.abs(levels - a[p, g]) >= 10]
            a[p, g + 8] = far[np.random.randint(len(far))]
    return np.exp2(a.ravel()).repeat(32)


def f64(x):
    return np.asarray(x).astype(np.float64)


def striped(idx):
    return np.tile(idx.reshape(-1, 16).T, (8, 1)).astype(np.uint16)


def unstriped(offs):
    return offs[:16].T.reshape(-1).astype(np.int64)


E2M1 = np.array([0.0, 0.5, 1.0, 1.5, 2.0, 3.0, 4.0, 6.0, -0.0, -0.5, -1.0, -1.5, -2.0, -3.0, -4.0, -6.0])


def pack_weight(w, fmt):
    k, n = w.shape
    w = f64(np.asarray(w, np.float32).astype(ml_dtypes.bfloat16)).reshape(k // 32, 32, n)
    amax = np.abs(w).max(1)
    if fmt == "e4m3":
        byte = np.frexp(amax)[1] - 1 + 127 - 7
    else:
        mant, ex = np.frexp(amax / 6.0)
        byte = np.where(mant > 0.5, ex, ex - 1) + 127
    byte = np.clip(np.where(amax > 0, byte, 1), 1, 254)
    scaled = (w * np.exp2(127.0 - byte)[:, None, :]).reshape(k, n).astype(np.float32)
    by_word = np.ascontiguousarray(scaled.reshape(k // 512, 128, 4, n).transpose(0, 1, 3, 2))
    if fmt == "e4m3":
        words = by_word.astype(ml_dtypes.float8_e4m3fn).view(np.uint8)
    else:
        c = by_word.astype(ml_dtypes.float4_e2m1fn).view(np.uint8) & 0xF
        words = (c[..., 0::2] | (c[..., 1::2] << 4)).reshape(k // 512, 128, 2 * n)
    return np.ascontiguousarray(words), np.ascontiguousarray(byte.astype(np.uint8).reshape(k // 512, 16, n))


def unpack_weight(words, scales, fmt):
    g, _, n = scales.shape
    words = np.ascontiguousarray(words).reshape(g, 128, n, -1)
    if fmt == "e4m3":
        vals = words.view(ml_dtypes.float8_e4m3fn).astype(np.float64)
    else:
        nib = np.empty((g, 128, n, 4), np.uint8)
        nib[..., 0::2] = words & 0xF
        nib[..., 1::2] = words >> 4
        vals = E2M1[nib]
    vals = vals * np.repeat(np.exp2(scales.astype(np.float64) - 127.0), 8, axis=1)[..., None]
    return vals.transpose(0, 1, 3, 2).reshape(g * 512, n)


def gelu(v):
    return 0.5 * v * (1.0 + np.tanh(np.sqrt(2.0 / np.pi) * (v + 0.044715 * v**3)))


def striped8(idx):
    return np.concatenate([v.reshape(-1, 16).T for v in idx]).astype(np.uint16)


def unstriped8(offs):
    return np.stack([offs[16 * g:16 * g + 16].T.reshape(-1) for g in range(8)]).astype(np.int64)


def runs(v, idx8):
    k = np.arange(v.shape[0])
    return v[k[:, None], idx8[k % 512 // 64]]


T, S, T2, K, M, H, N = 2048, 1024, 2048, 1024, 512, 1024, 512


def setup_inputs():
    n = np.random.standard_normal
    s1 = mx_kscale(K)[:, None]
    s2 = mx_kscale(M)[:, None]
    u = mx_kscale(H)[:, None]
    tab_words, tab_scales = pack_weight(n((K, T)) * s1, "e4m3")
    tab2_words, tab2_scales = pack_weight(n((M, T)) * s2, "e4m3")
    wb_words, wb_scales = pack_weight(1.4 * n((M, H)) / np.sqrt(M) / s2 * u.T, "e2m1")
    wo_words, wo_scales = pack_weight(1.4 * n((H, N)) / np.sqrt(H) / u, "e4m3")
    return {
        "tab_words": tab_words, "tab_scales": tab_scales,
        "tab2_words": tab2_words, "tab2_scales": tab2_scales,
        "offs": striped8(np.stack([np.random.permutation(T)[:S] for _ in range(8)])),
        "offs2": striped(np.random.permutation(T)[:S]),
        "offs3": striped(np.random.permutation(T2)[:S]),
        "w1": (0.54 * n((K, H)) / np.sqrt(K) / s1).astype(np.float32),
        "wb_words": wb_words, "wb_scales": wb_scales,
        "wd": (1.3 * n((M, H)) / np.sqrt(M) / s2).astype(np.float32),
        "gd": (np.random.uniform(0.6, 1.2, H) * u[:, 0]).astype(np.float32),
        "wo_words": wo_words, "wo_scales": wo_scales,
        "page1": (0.6 * n((N, T2))).astype(np.float32),
        "wgo": np.exp(0.3 * n((128, S))).astype(np.float32),
    }


def reference(tab_words, tab_scales, tab2_words, tab2_scales, offs, offs2, offs3,
              w1, wb_words, wb_scales, wd, gd, wo_words, wo_scales, page1, wgo):
    v = runs(unpack_weight(tab_words, tab_scales, "e4m3"), unstriped8(offs))
    v2 = unpack_weight(tab2_words, tab2_scales, "e4m3")[:, unstriped(offs2)]
    f = mxq(f64(w1), 0, "e4m3").T @ v
    b = unpack_weight(wb_words, wb_scales, "e2m1").T @ v2
    d = mxq(f64(wd), 0, "e4m3").T @ v2
    h = np.maximum(np.sin(f) * b, f64(gd)[:, None] * np.tanh(d))
    y = unpack_weight(wo_words, wo_scales, "e4m3").T @ mxq(h, 0, "e4m3")
    out = f64(page1).copy()
    out[:, unstriped(offs3)] = np.tile(f64(wgo), (N // 128, 1)) * y
    return out

@@ -1,0 +1,283 @@
+import math
+from contextlib import ExitStack
+
+import concourse.mybir as mybir
+
+T, S, K, M, H, N = 2048, 1024, 1024, 512, 1024, 512
+FLOPS = 2 * S * (K * H + 2 * M * H + H * N)
+
+F32 = mybir.dt.float32
+BF16 = mybir.dt.bfloat16
+I32 = mybir.dt.int32
+U32 = mybir.dt.uint32
+U16 = mybir.dt.uint16
+U8 = mybir.dt.uint8
+FP8X4 = mybir.dt.float8_e4m3fn_x4
+FP4X4 = mybir.dt.float4_e2m1fn_x4
+ALU = mybir.AluOpType
+ACT = mybir.ActivationFunctionType
+
+P = 128
+PASS = 512
+BLOCK = 256
+GATHER = 512
+MAGIC = 1.5 * 2.0**23
+
+
+def tile_list_scratch_repair_ranker_kernel(
+    tc, tab_words, tab_scales, tab2_words, tab2_scales, offs, offs2, offs3,
+    w1, wb_words, wb_scales, wd, gd, wo_words, wo_scales, page1, wgo, out,
+):
+    nc = tc.nc
+    with ExitStack() as ctx:
+        keep = ctx.enter_context(tc.tile_pool(name="keep", bufs=1))
+        stage = ctx.enter_context(tc.tile_pool(name="stage", bufs=3))
+        psum = ctx.enter_context(tc.psum_pool(name="psum", bufs=1))
+
+        def zeroed_bytes(name, width):
+            tile = keep.tile([P, width], U8, name=name, align_bytes=64)
+            nc.vector.memset(tile[:].bitcast(I32), 0)
+            return tile
+
+        def load_list(name, src):
+            tile = keep.tile([P, S // 16], U16, name=name)
+            nc.sync.dma_start(tile[:], src)
+            return tile
+
+        def load_words(name, src):
+            tile = keep.tile([P, src.shape[1]], I32, name=name, align_bytes=64)
+            nc.sync.dma_start(tile[:], src.rearrange("p c i -> p (c i)").bitcast(I32))
+            return tile
+
+        def load_plane(tile, src):
+            for d in range(4):
+                nc.sync.dma_start(tile[32 * d : 32 * d + 4, :].bitcast(I32), src[4 * d : 4 * d + 4, :].bitcast(I32))
+
+        def load_weight(src, kp, a):
+            raw = stage.tile([P, 4, PASS], F32, name="raw", bufs=4)
+            rows = src[PASS * kp : PASS * (kp + 1), PASS * a : PASS * (a + 1)]
+            nc.sync.dma_start(raw[:], rows.rearrange("(p j) c -> p j c", j=4))
+            return raw
+
+        def quantise_weight(name, raw, on_vector):
+            grouped = stage.tile([P, 4 * PASS], BF16, name="grouped", bufs=2, align_bytes=64)
+            dst = grouped[:].rearrange("p (t m j) -> p m t j", t=4, j=4)
+            src = raw[:].rearrange("p j (m t) -> p m t j", t=4)
+            if on_vector:
+                nc.vector.tensor_copy(dst[:, :on_vector], src[:, :on_vector])
+            if on_vector < P:
+                nc.scalar.copy(dst[:, on_vector:], src[:, on_vector:])
+            codes = keep.tile([P, PASS], U32, name=name + "_codes", align_bytes=64)
+            plane = keep.tile([P, PASS], U8, name=name + "_plane", align_bytes=64)
+            nc.vector.quantize_mx(codes[:].bitcast(FP8X4), plane[:], grouped[:])
+            return codes, plane
+
+        def gather_words(name, table, lst, g):
+            picked = keep.tile([P, GATHER], U32, name=name, align_bytes=64)
+            cols = slice(g * GATHER // 16, (g + 1) * GATHER // 16)
+            nc.vector.tensor_copy(picked[:], table[:].bitcast(U32).indirect(lst[:, cols]))
+            return picked
+
+        tab_rows = zeroed_bytes("tab_rows", T)
+        tab2_rows = zeroed_bytes("tab2_rows", T)
+        list2 = load_list("list2", offs2)
+        list1 = load_list("list1", offs)
+        load_plane(tab2_rows, tab2_scales[0])
+        table2 = load_words("table2", tab2_words[0])
+        raw_wd = [load_weight(wd, 0, 0)]
+        for a in range(2):
+            for b in range(2):
+                src = tab_scales[a].rearrange("(g b) t -> b g t", b=2)[b]
+                nc.sync.dma_start(tab_rows[4 * a + b : P : 16, :].bitcast(I32), src.bitcast(I32))
+        raw_wd.append(load_weight(wd, 0, 1))
+        table = [load_words("table0", tab_words[0])]
+        raw_w1 = {(0, 0): load_weight(w1, 0, 0)}
+        table.append(load_words("table1", tab_words[1]))
+
+        v2_plane = keep.tile([P, S], U8, name="v2_plane", align_bytes=64)
+        nc.vector.tensor_copy(v2_plane[:], tab2_rows[:].indirect(list2[:]))
+        v2 = {g: gather_words("v2_%d" % g, table2, list2, g) for g in range(2)}
+        wdq = {0: quantise_weight("wd_0", raw_wd[0], 0)}
+        v_rows = keep.tile([P, S], U8, name="v_rows", align_bytes=64)
+        nc.vector.tensor_copy(v_rows[:], tab_rows[:].indirect(list1[:]))
+        v_plane = keep.tile([P, S], U8, name="v_plane", align_bytes=64)
+        nc.vector.tensor_copy(v_plane[:].bitcast(I32), v_rows[:].bitcast(I32))
+        wdq[1] = quantise_weight("wd_1", raw_wd[1], 0)
+        raw_w1[1, 0] = load_weight(w1, 1, 0)
+        for a in range(2):
+            for b in range(2):
+                nc.sync.dma_start(
+                    v_plane[4 * a + 2 + b : P : 32, :].bitcast(I32),
+                    v_rows[16 + 4 * a + b : P : 32, :].bitcast(I32),
+                )
+        wb_raw = keep.tile([P, 2 * H], U8, name="wb_raw")
+        nc.sync.dma_start(wb_raw[:].bitcast(I32), wb_words[0].bitcast(I32))
+        wb_rows = zeroed_bytes("wb_rows", H)
+        load_plane(wb_rows, wb_scales[0])
+        gains = keep.tile([P, 2, 4], F32, name="gains")
+        nc.sync.dma_start(gains[:], gd.rearrange("(a p t) -> p a t", a=2, t=4))
+        raw_w1[0, 1] = load_weight(w1, 0, 1)
+        raw_w1[1, 1] = load_weight(w1, 1, 1)
+        wo_codes = [load_words("wo%d" % a, wo_words[a]) for a in range(2)]
+        wo_plane = zeroed_bytes("wo_plane", N)
+        for d in range(4):
+            nc.sync.dma_start(
+                wo_plane[32 * d : 32 * d + 8, :].bitcast(I32), wo_scales[:, 4 * d : 4 * d + 4, :].bitcast(I32)
+            )
+        list3 = load_list("list3", offs3)
+        gate = keep.tile([P, S], F32, name="gate")
+        nc.sync.dma_start(gate[:], wgo)
+        page = []
+        for u in range(N // P):
+            page.append(keep.tile([P, T], F32, name="page%d" % u))
+            nc.sync.dma_start(page[u][:], page1[P * u : P * (u + 1), :])
+
+        steps = [(jb, a, tp) for jb in range(S // BLOCK) for a in range(2) for tp in range(2)]
+        held = {}
+        planar = {}
+        hq = {}
+        wide = 2 * BLOCK
+
+        def first_stage(name, bufs, i, passes):
+            jb, a, tp = steps[i]
+            g, c0 = divmod(BLOCK * jb, GATHER)
+            bank = psum.tile([P, wide], F32, name=name, bufs=bufs)
+            for s in range(2):
+                operands = passes(a, 2 * tp + s, g)
+                for n, (codes, plane, words, words_plane) in enumerate(operands):
+                    nc.tensor.matmul_mx(
+                        bank[:, BLOCK * s : BLOCK * (s + 1)], lhsT=codes, lhsT_scale=plane,
+                        rhs=words[:, c0 : c0 + BLOCK].bitcast(FP8X4),
+                        rhs_scale=words_plane[:, BLOCK * jb : BLOCK * (jb + 1)],
+                        start=(n == 0), stop=(n == len(operands) - 1),
+                    )
+            return bank
+
+        def frame_passes(a, t, g):
+            c = slice(P * t, P * (t + 1))
+            return [
+                (w1q[kp, a][0][:, c].bitcast(FP8X4), w1q[kp, a][1][:, c], v[kp, g], v_plane[4 * kp :, :])
+                for kp in range(2)
+            ]
+
+        def wd_passes(a, t, g):
+            c = slice(P * t, P * (t + 1))
+            return [(wdq[a][0][:, c].bitcast(FP8X4), wdq[a][1][:, c], v2[g], v2_plane[:])]
+
+        def wb_passes(a, t, g):
+            c0 = PASS * a + P * t
+            return [(wb_codes[:, 2 * c0 : 2 * (c0 + P)].bitcast(FP4X4), wb_plane[:, c0 : c0 + P], v2[g], v2_plane[:])]
+
+        def reduce_angle(i):
+            f = first_stage("f", 3, i, frame_passes)
+            turns = stage.tile([P, wide], F32, name="turns", bufs=3)
+            nc.scalar.activation(turns[:], f[:], ACT.Copy, bias=0.0, scale=1.0 / (2.0 * math.pi))
+            whole = stage.tile([P, wide], I32, name="whole", bufs=3)
+            nc.scalar.activation(whole[:].bitcast(U32), f[:], ACT.Copy, bias=MAGIC, scale=1.0 / (2.0 * math.pi))
+            rest = stage.tile([P, wide], F32, name="rest", bufs=3)
+            nc.vector.scalar_tensor_tensor(rest[:], whole[:], MAGIC, turns[:], ALU.subtract, ALU.subtract)
+            held["rest", i] = rest
+
+        def product(i):
+            sin = stage.tile([P, wide], F32, name="sin", bufs=3)
+            nc.scalar.activation(sin[:], held["rest", i][:], ACT.Sin, scale=-2.0 * math.pi)
+            b = first_stage("b", 3, i, wb_passes)
+            prod = stage.tile([P, wide], F32, name="prod", bufs=3)
+            nc.vector.tensor_tensor(prod[:], sin[:], b[:], ALU.mult)
+            held["prod", i] = prod
+
+        def donor_tanh(i):
+            d = first_stage("dy", 2, i, wd_passes)
+            tanh = keep.tile([P, wide], F32, name="tanh%d" % i)
+            nc.scalar.activation(tanh[:], d[:], ACT.Tanh)
+            held["tanh", i] = tanh
+
+        def larger(i):
+            jb, a, tp = steps[i]
+            tanh = held["tanh", i]
+            if tp == 0:
+                planar[jb, a] = stage.tile([P, 4, BLOCK], BF16, name="planar", bufs=3)
+            for s in range(2):
+                t = 2 * tp + s
+                c = slice(BLOCK * s, BLOCK * (s + 1))
+                nc.vector.scalar_tensor_tensor(
+                    planar[jb, a][:, t, :], tanh[:, c], gains[:, a, t : t + 1], held["prod", i][:, c], ALU.mult, ALU.max
+                )
+
+        def weave(jb, a, on_vector):
+            woven = stage.tile([P, 4 * BLOCK], BF16, name="woven", bufs=3, align_bytes=64)
+            dst = woven[:].rearrange("p (c i t) -> p c t i", i=4, t=4)
+            src = planar[jb, a][:].rearrange("p t (c i) -> p c t i", i=4)
+            if on_vector:
+                nc.vector.tensor_copy(dst, src)
+            else:
+                nc.scalar.copy(dst, src)
+            held["woven", jb, a] = woven
+
+        def quantise_h(jb, a):
+            codes = stage.tile([P, BLOCK], U32, name="h_codes", bufs=4, align_bytes=64)
+            plane = stage.tile([P, BLOCK], U8, name="h_plane", bufs=4, align_bytes=64)
+            nc.vector.quantize_mx(codes[:].bitcast(FP8X4), plane[:], held["woven", jb, a][:])
+            hq[jb, a] = (codes, plane)
+
+        def second_stage(jb, u):
+            y = psum.tile([P, BLOCK], F32, name="dy", bufs=2)
+            ucols = slice(P * u, P * (u + 1))
+            for a in range(2):
+                codes, plane = hq[jb, a]
+                nc.tensor.matmul_mx(
+                    y[:], lhsT=wo_codes[a][:, ucols].bitcast(FP8X4), lhsT_scale=wo_plane[4 * a :, ucols],
+                    rhs=codes[:].bitcast(FP8X4), rhs_scale=plane[:], start=(a == 0), stop=(a == 1),
+                )
+            y_sb = stage.tile([P, BLOCK], F32, name="y_sb", bufs=4)
+            nc.scalar.copy(y_sb[:], y[:])
+            lst = list3[:, BLOCK * jb // 16 : BLOCK * (jb + 1) // 16]
+            nc.vector.tensor_tensor(page[u][:].indirect(lst), y_sb[:], gate[:, BLOCK * jb : BLOCK * (jb + 1)], ALU.mult)
+            if jb == S // BLOCK - 1:
+                nc.sync.dma_start(out[P * u : P * (u + 1), :], page[u][:])
+
+        count = len(steps)
+        LAG = 1
+        for a in range(2):
+            for i in range(count):
+                if steps[i][1] == a:
+                    donor_tanh(i)
+        v = {}
+        v[0, 0] = gather_words("v00", table[0], list1, 0)
+        w1q = {(0, 0): quantise_weight("w1_00", raw_w1[0, 0], 128)}
+        v[1, 0] = gather_words("v10", table[1], list1, 0)
+        w1q[1, 0] = quantise_weight("w1_10", raw_w1[1, 0], 128)
+        wb_codes = keep.tile([P, 2 * H], U8, name="wb_codes", align_bytes=64)
+        nc.vector.tensor_copy(
+            wb_codes[:].bitcast(U16).rearrange("p (a t m) -> p a m t", a=2, t=4),
+            wb_raw[:].bitcast(U16).rearrange("p (a m t) -> p a m t", a=2, t=4),
+        )
+        wb_plane = keep.tile([P, H], U8, name="wb_plane", align_bytes=64)
+        nc.vector.tensor_copy(
+            wb_plane[:].rearrange("p (a t m) -> p a t m", a=2, t=4),
+            wb_rows[:].rearrange("p (a m t) -> p a t m", a=2, t=4),
+        )
+        for step in range(count + LAG + 9):
+            if step == 1:
+                w1q[0, 1] = quantise_weight("w1_01", raw_w1[0, 1], 0)
+            if step == 2:
+                w1q[1, 1] = quantise_weight("w1_11", raw_w1[1, 1], 64)
+            if step == 5:
+                v[0, 1] = gather_words("v01", table[0], list1, 1)
+            if step == 6:
+                v[1, 1] = gather_words("v11", table[1], list1, 1)
+            if step < count:
+                reduce_angle(step)
+            if 0 <= step - LAG < count:
+                product(step - LAG)
+            if 0 <= step - LAG - 1 < count:
+                larger(step - LAG - 1)
+            i = step - LAG - 2
+            if 0 <= i < count and i % 2 == 1:
+                weave(steps[i][0], steps[i][1], i == count - 1)
+            i = step - LAG - 3
+            if 0 <= i < count and i % 2 == 1:
+                quantise_h(steps[i][0], steps[i][1])
+            i = step - LAG - 7
+            if 0 <= i < count:
+                second_stage(i // 4, i % 4)

@@ -2,6 +2,7 @@ import math
 from contextlib import ExitStack
 
 import concourse.mybir as mybir
+from concourse.masks import make_identity
 
 T, S, K, M, H, N = 2048, 1024, 1024, 512, 1024, 512
 FLOPS = 2 * S * (K * H + 2 * M * H + H * N)
@@ -19,9 +20,17 @@ ACT = mybir.ActivationFunctionType
 
 P = 128
 PASS = 512
+HALF = S // 2
 BLOCK = 256
-GATHER = 512
-MAGIC = 1.5 * 2.0**23
+BLOCKS = S // BLOCK
+PAGES = N // P
+
+OFFSET = 1.5 * 2.0**16
+OFFSET_BITS = float(0x47C00000)
+
+AHEAD = 3
+TURN_BUFS = AHEAD + 2
+EARLY_WEAVES = 3
 
 
 def tile_list_scratch_repair_ranker_kernel(
@@ -32,9 +41,9 @@ def tile_list_scratch_repair_ranker_kernel(
     with ExitStack() as ctx:
         keep = ctx.enter_context(tc.tile_pool(name="keep", bufs=1))
         stage = ctx.enter_context(tc.tile_pool(name="stage", bufs=3))
-        psum = ctx.enter_context(tc.psum_pool(name="psum", bufs=1))
+        psum = ctx.enter_context(tc.psum_pool(name="psum", bufs=2))
 
-        def zeroed_bytes(name, width):
+        def zeroed_scale_tile(name, width):
             tile = keep.tile([P, width], U8, name=name, align_bytes=64)
             nc.vector.memset(tile[:].bitcast(I32), 0)
             return tile
@@ -49,235 +58,258 @@ def tile_list_scratch_repair_ranker_kernel(
             nc.sync.dma_start(tile[:], src.rearrange("p c i -> p (c i)").bitcast(I32))
             return tile
 
-        def load_plane(tile, src):
+        def load_scale_rows(tile, src):
             for d in range(4):
                 nc.sync.dma_start(tile[32 * d : 32 * d + 4, :].bitcast(I32), src[4 * d : 4 * d + 4, :].bitcast(I32))
 
         def load_weight(src, kp, a):
-            raw = stage.tile([P, 4, PASS], F32, name="raw", bufs=4)
+            raw = stage.tile([P, 4, PASS], F32, name="raw", bufs=4, align_bytes=64)
             rows = src[PASS * kp : PASS * (kp + 1), PASS * a : PASS * (a + 1)]
             nc.sync.dma_start(raw[:], rows.rearrange("(p j) c -> p j c", j=4))
             return raw
 
-        def quantise_weight(name, raw, on_vector):
-            grouped = stage.tile([P, 4 * PASS], BF16, name="grouped", bufs=2, align_bytes=64)
-            dst = grouped[:].rearrange("p (t m j) -> p m t j", t=4, j=4)
-            src = raw[:].rearrange("p j (m t) -> p m t j", t=4)
-            if on_vector:
-                nc.vector.tensor_copy(dst[:, :on_vector], src[:, :on_vector])
-            if on_vector < P:
-                nc.scalar.copy(dst[:, on_vector:], src[:, on_vector:])
-            codes = keep.tile([P, PASS], U32, name=name + "_codes", align_bytes=64)
-            plane = keep.tile([P, PASS], U8, name=name + "_plane", align_bytes=64)
-            nc.vector.quantize_mx(codes[:].bitcast(FP8X4), plane[:], grouped[:])
-            return codes, plane
+        def rounded_buffer(shape, dtype):
+            return stage.tile(shape, dtype, name="rounded", bufs=2, align_bytes=64)
 
-        def gather_words(name, table, lst, g):
-            picked = keep.tile([P, GATHER], U32, name=name, align_bytes=64)
-            cols = slice(g * GATHER // 16, (g + 1) * GATHER // 16)
-            nc.vector.tensor_copy(picked[:], table[:].bitcast(U32).indirect(lst[:, cols]))
+        def quantise_weight(name, raw, cast):
+            rounded = rounded_buffer([P, 4 * PASS], BF16)
+            cast(
+                rounded[:].rearrange("p (h e m j) -> p h m j e", h=2, e=2, j=4),
+                raw[:].rearrange("p j (m h e) -> p h m j e", h=2, e=2),
+            )
+            codes = keep.tile([P, PASS], U32, name=name + "_codes", align_bytes=64)
+            scales = keep.tile([P, PASS], U8, name=name + "_scales", align_bytes=64)
+            nc.vector.quantize_mx(codes[:].bitcast(FP8X4), scales[:], rounded[:])
+            return codes, scales
+
+        def gather_words(picked, table, offsets, half):
+            cols = slice(half * HALF // 16, (half + 1) * HALF // 16)
+            nc.vector.tensor_copy(picked[:], table[:].bitcast(U32).indirect(offsets[:, cols]))
             return picked
 
-        tab_rows = zeroed_bytes("tab_rows", T)
-        tab2_rows = zeroed_bytes("tab2_rows", T)
-        list2 = load_list("list2", offs2)
-        list1 = load_list("list1", offs)
-        load_plane(tab2_rows, tab2_scales[0])
-        table2 = load_words("table2", tab2_words[0])
-        raw_wd = [load_weight(wd, 0, 0)]
-        for a in range(2):
-            for b in range(2):
-                src = tab_scales[a].rearrange("(g b) t -> b g t", b=2)[b]
-                nc.sync.dma_start(tab_rows[4 * a + b : P : 16, :].bitcast(I32), src.bitcast(I32))
-        raw_wd.append(load_weight(wd, 0, 1))
-        table = [load_words("table0", tab_words[0])]
-        raw_w1 = {(0, 0): load_weight(w1, 0, 0)}
-        table.append(load_words("table1", tab_words[1]))
+        def kept_words(name):
+            return keep.tile([P, HALF], U32, name=name, align_bytes=64)
 
-        v2_plane = keep.tile([P, S], U8, name="v2_plane", align_bytes=64)
-        nc.vector.tensor_copy(v2_plane[:], tab2_rows[:].indirect(list2[:]))
-        v2 = {g: gather_words("v2_%d" % g, table2, list2, g) for g in range(2)}
-        wdq = {0: quantise_weight("wd_0", raw_wd[0], 0)}
-        v_rows = keep.tile([P, S], U8, name="v_rows", align_bytes=64)
-        nc.vector.tensor_copy(v_rows[:], tab_rows[:].indirect(list1[:]))
-        v_plane = keep.tile([P, S], U8, name="v_plane", align_bytes=64)
-        nc.vector.tensor_copy(v_plane[:].bitcast(I32), v_rows[:].bitcast(I32))
-        wdq[1] = quantise_weight("wd_1", raw_wd[1], 0)
-        raw_w1[1, 0] = load_weight(w1, 1, 0)
-        for a in range(2):
-            for b in range(2):
-                nc.sync.dma_start(
-                    v_plane[4 * a + 2 + b : P : 32, :].bitcast(I32),
-                    v_rows[16 + 4 * a + b : P : 32, :].bitcast(I32),
+        units = [(0, 0), (1, 0), (0, 1), (1, 1)] + [(jb, a) for jb in range(2, BLOCKS) for a in range(2)]
+        steps = [(jb, a, part) for jb, a in units for part in range(2)]
+        count = len(steps)
+        wide = 2 * BLOCK
+        table, v, v2, w1q, wdq = {}, {}, {}, {}, {}
+        tanh, turns, offset_less_whole, prod, planes, woven, hq = {}, {}, {}, {}, {}, {}, {}
+
+        def donor_product(bank_name, i, weight_columns):
+            jb, a, part = steps[i]
+            half, c0 = divmod(BLOCK * jb, HALF)
+            bank = psum.tile([P, wide], F32, name=bank_name)
+            for s in range(2):
+                codes, scales = weight_columns(a, 2 * part + s)
+                nc.tensor.matmul_mx(
+                    bank[:, BLOCK * s : BLOCK * (s + 1)], lhsT=codes, lhsT_scale=scales,
+                    rhs=v2[half][:, c0 : c0 + BLOCK].bitcast(FP8X4),
+                    rhs_scale=v2_scales[:, BLOCK * jb : BLOCK * (jb + 1)], start=True, stop=True,
                 )
-        wb_raw = keep.tile([P, 2 * H], U8, name="wb_raw")
-        nc.sync.dma_start(wb_raw[:].bitcast(I32), wb_words[0].bitcast(I32))
-        wb_rows = zeroed_bytes("wb_rows", H)
-        load_plane(wb_rows, wb_scales[0])
+            return bank
+
+        def wd_columns(a, t):
+            c = slice(P * t, P * (t + 1))
+            return wdq[a][0][:, c].bitcast(FP8X4), wdq[a][1][:, c]
+
+        def wb_columns(a, t):
+            c0 = PASS * a + P * t
+            return wb_codes[:, 2 * c0 : 2 * (c0 + P)].bitcast(FP4X4), wb_scale_tile[:, c0 : c0 + P]
+
+        def donor_tanh(i):
+            d = donor_product(("y", "b")[i % 2], i, wd_columns)
+            tanh[i] = keep.tile([P, wide], F32, name="tanh%d" % i)
+            nc.scalar.activation(tanh[i][:], d[:], ACT.Tanh)
+
+        def count_turns(i):
+            jb, a, part = steps[i]
+            j0 = BLOCK * jb + P * part
+            half, c0 = divmod(j0, HALF)
+            f = psum.tile([P, PASS], F32, name="f")
+            for kp in range(2):
+                nc.tensor.matmul_mx(
+                    f[:], lhsT=v[kp, half][:, c0 : c0 + P].bitcast(FP8X4), lhsT_scale=v_scales[4 * kp :, j0 : j0 + P],
+                    rhs=w1q[kp, a][0][:].bitcast(FP8X4), rhs_scale=w1q[kp, a][1][:], start=(kp == 0), stop=(kp == 1),
+                )
+            turns[i] = stage.tile([P, PASS], F32, name="turns", bufs=TURN_BUFS)
+            nc.scalar.activation(turns[i][:], f[:], ACT.Copy, bias=0.0, scale=1.0 / (2.0 * math.pi))
+            offset_less_whole[i] = stage.tile([P, PASS], U32, name="offset_less_whole", bufs=TURN_BUFS)
+            nc.scalar.activation(offset_less_whole[i][:], f[:], ACT.Copy, bias=OFFSET_BITS, scale=-128.0 / (2.0 * math.pi))
+
+        def sine_times_b(i):
+            jb, a, part = steps[i]
+            rest = psum.tile([P, wide], F32, name="rest")
+            for s in range(2):
+                c = slice(P * (2 * part + s), P * (2 * part + s + 1))
+                for entries in range(2):
+                    source = i - part + entries
+                    terms = [offset_less_whole[source][:].bitcast(F32)[:, c], minus_offset[:], turns[source][:, c]]
+                    for n, term in enumerate(terms):
+                        nc.tensor.matmul(
+                            rest[:, BLOCK * s + P * entries : BLOCK * s + P * (entries + 1)], lhsT=term, rhs=ident[:],
+                            is_transpose=True, start=(n == 0), stop=(n == len(terms) - 1),
+                        )
+            sine = stage.tile([P, wide], F32, name="sine", bufs=4)
+            nc.scalar.activation(sine[:], rest[:], ACT.Sin, scale=2.0 * math.pi)
+            b = donor_product("b", i, wb_columns)
+            prod[i] = stage.tile([P, wide], F32, name="prod")
+            for s in range(2):
+                c = slice(BLOCK * s, BLOCK * (s + 1))
+                nc.vector.tensor_tensor(prod[i][:, c], sine[:, c], b[:, c], ALU.mult)
+
+        def larger(i):
+            jb, a, part = steps[i]
+            if (jb, a, part) == (*units[-1], 0):
+                planes[jb, a] = stage.tile([P, 4, BLOCK], BF16, name="last_planes", bufs=1)
+            elif part == 0:
+                planes[jb, a] = stage.tile([P, 4, BLOCK], BF16, name="planes")
+            for s in range(2):
+                t = 2 * part + s
+                c = slice(BLOCK * s, BLOCK * (s + 1))
+                nc.vector.scalar_tensor_tensor(
+                    planes[jb, a][:, t, :], tanh[i][:, c], gains[:, a, t : t + 1], prod[i][:, c], ALU.mult, ALU.max
+                )
+
+        def weave(unit, copy):
+            woven[unit] = stage.tile([P, 4 * BLOCK], BF16, name="woven", align_bytes=64)
+            copy(
+                woven[unit][:].rearrange("p (c i t) -> p c t i", i=4, t=4),
+                planes[unit][:].rearrange("p t (c i) -> p c t i", i=4),
+            )
+
+        def quantise_h(unit):
+            codes = stage.tile([P, BLOCK], U32, name="h_codes", bufs=5, align_bytes=64)
+            scales = stage.tile([P, BLOCK], U8, name="h_scales", bufs=5, align_bytes=64)
+            nc.vector.quantize_mx(codes[:].bitcast(FP8X4), scales[:], woven[unit][:])
+            hq[unit] = (codes, scales)
+
+        def place(jb, u):
+            y = psum.tile([P, BLOCK], F32, name="y")
+            c = slice(P * u, P * (u + 1))
+            for a in range(2):
+                codes, scales = hq[jb, a]
+                nc.tensor.matmul_mx(
+                    y[:], lhsT=wo_codes[a][:, c].bitcast(FP8X4), lhsT_scale=wo_scale_tile[4 * a :, c],
+                    rhs=codes[:].bitcast(FP8X4), rhs_scale=scales[:], start=(a == 0), stop=(a == 1),
+                )
+            if (jb, u) == filler:
+                y_sb = stage.tile([P, BLOCK], F32, name="last_planes", bufs=1)
+            else:
+                y_sb = stage.tile([P, BLOCK], F32, name="y_sb", bufs=PAGES)
+            nc.scalar.copy(y_sb[:], y[:])
+            offsets = list3[:, BLOCK * jb // 16 : BLOCK * (jb + 1) // 16]
+            nc.vector.tensor_tensor(page[u][:].indirect(offsets), y_sb[:], gate[:, BLOCK * jb : BLOCK * (jb + 1)], ALU.mult)
+            if jb == BLOCKS - 1:
+                nc.sync.dma_start(out[P * u : P * (u + 1), :], page[u][:])
+
+        ident = keep.tile([P, P], F32, name="ident")
+        make_identity(nc, ident[:])
+        minus_offset = keep.tile([P, P], F32, name="minus_offset")
+        nc.gpsimd.memset(minus_offset[:], -OFFSET)
+        tab2_rows = zeroed_scale_tile("tab2_rows", T)
+        tab_rows = zeroed_scale_tile("tab_rows", T)
+        wb_rows = zeroed_scale_tile("wb_rows", H)
+        wo_scale_tile = zeroed_scale_tile("wo_scale_tile", N)
+
+        list1 = load_list("list1", offs)
+        list2 = load_list("list2", offs2)
+        list3 = load_list("list3", offs3)
         gains = keep.tile([P, 2, 4], F32, name="gains")
         nc.sync.dma_start(gains[:], gd.rearrange("(a p t) -> p a t", a=2, t=4))
+        table2 = load_words("table2", tab2_words[0])
+        wb_raw = keep.tile([P, 2 * H], U8, name="wb_raw")
+        nc.sync.dma_start(wb_raw[:].bitcast(I32), wb_words[0].bitcast(I32))
+        load_scale_rows(tab2_rows, tab2_scales[0])
+        raw_wd = [load_weight(wd, 0, 0)]
+        for kp in range(2):
+            for odd in range(2):
+                src = tab_scales[kp].rearrange("(g odd) t -> odd g t", odd=2)[odd]
+                nc.sync.dma_start(tab_rows[4 * kp + odd : P : 16, :].bitcast(I32), src.bitcast(I32))
+        raw_wd.append(load_weight(wd, 0, 1))
+        table[0] = load_words("table0", tab_words[0])
+        raw_w1 = {(0, 0): load_weight(w1, 0, 0)}
+        table[1] = load_words("table1", tab_words[1])
+
+        v2[0] = gather_words(kept_words("v2_0"), table2, list2, 0)
+        v2_scales = keep.tile([P, S], U8, name="v2_scales", align_bytes=64)
+        nc.vector.tensor_copy(v2_scales[:], tab2_rows[:].indirect(list2[:]))
+        v2[1] = gather_words(kept_words("v2_1"), table2, list2, 1)
+        wdq[0] = quantise_weight("wd_0", raw_wd[0], nc.scalar.copy)
+        v_rows = keep.tile([P, S], U8, name="v_rows", align_bytes=64)
+        nc.vector.tensor_copy(v_rows[:], tab_rows[:].indirect(list1[:]))
+        v_scales = keep.tile([P, S], U8, name="v_scales", align_bytes=64)
+        nc.vector.tensor_copy(v_scales[:].bitcast(I32), v_rows[:].bitcast(I32))
+        wdq[1] = quantise_weight("wd_1", raw_wd[1], nc.scalar.copy)
+        raw_w1[1, 0] = load_weight(w1, 1, 0)
+        for kp in range(2):
+            for odd in range(2):
+                nc.sync.dma_start(
+                    v_scales[4 * kp + 2 + odd : P : 32, :].bitcast(I32),
+                    v_rows[16 + 4 * kp + odd : P : 32, :].bitcast(I32),
+                )
         raw_w1[0, 1] = load_weight(w1, 0, 1)
         raw_w1[1, 1] = load_weight(w1, 1, 1)
+        load_scale_rows(wb_rows, wb_scales[0])
         wo_codes = [load_words("wo%d" % a, wo_words[a]) for a in range(2)]
-        wo_plane = zeroed_bytes("wo_plane", N)
         for d in range(4):
             nc.sync.dma_start(
-                wo_plane[32 * d : 32 * d + 8, :].bitcast(I32), wo_scales[:, 4 * d : 4 * d + 4, :].bitcast(I32)
+                wo_scale_tile[32 * d : 32 * d + 8, :].bitcast(I32), wo_scales[:, 4 * d : 4 * d + 4, :].bitcast(I32)
             )
-        list3 = load_list("list3", offs3)
         gate = keep.tile([P, S], F32, name="gate")
         nc.sync.dma_start(gate[:], wgo)
         page = []
-        for u in range(N // P):
+        for u in range(PAGES):
             page.append(keep.tile([P, T], F32, name="page%d" % u))
             nc.sync.dma_start(page[u][:], page1[P * u : P * (u + 1), :])
 
-        steps = [(jb, a, tp) for jb in range(S // BLOCK) for a in range(2) for tp in range(2)]
-        held = {}
-        planar = {}
-        hq = {}
-        wide = 2 * BLOCK
-
-        def first_stage(name, bufs, i, passes):
-            jb, a, tp = steps[i]
-            g, c0 = divmod(BLOCK * jb, GATHER)
-            bank = psum.tile([P, wide], F32, name=name, bufs=bufs)
-            for s in range(2):
-                operands = passes(a, 2 * tp + s, g)
-                for n, (codes, plane, words, words_plane) in enumerate(operands):
-                    nc.tensor.matmul_mx(
-                        bank[:, BLOCK * s : BLOCK * (s + 1)], lhsT=codes, lhsT_scale=plane,
-                        rhs=words[:, c0 : c0 + BLOCK].bitcast(FP8X4),
-                        rhs_scale=words_plane[:, BLOCK * jb : BLOCK * (jb + 1)],
-                        start=(n == 0), stop=(n == len(operands) - 1),
-                    )
-            return bank
-
-        def frame_passes(a, t, g):
-            c = slice(P * t, P * (t + 1))
-            return [
-                (w1q[kp, a][0][:, c].bitcast(FP8X4), w1q[kp, a][1][:, c], v[kp, g], v_plane[4 * kp :, :])
-                for kp in range(2)
-            ]
-
-        def wd_passes(a, t, g):
-            c = slice(P * t, P * (t + 1))
-            return [(wdq[a][0][:, c].bitcast(FP8X4), wdq[a][1][:, c], v2[g], v2_plane[:])]
-
-        def wb_passes(a, t, g):
-            c0 = PASS * a + P * t
-            return [(wb_codes[:, 2 * c0 : 2 * (c0 + P)].bitcast(FP4X4), wb_plane[:, c0 : c0 + P], v2[g], v2_plane[:])]
-
-        def reduce_angle(i):
-            f = first_stage("f", 3, i, frame_passes)
-            turns = stage.tile([P, wide], F32, name="turns", bufs=3)
-            nc.scalar.activation(turns[:], f[:], ACT.Copy, bias=0.0, scale=1.0 / (2.0 * math.pi))
-            whole = stage.tile([P, wide], I32, name="whole", bufs=3)
-            nc.scalar.activation(whole[:].bitcast(U32), f[:], ACT.Copy, bias=MAGIC, scale=1.0 / (2.0 * math.pi))
-            rest = stage.tile([P, wide], F32, name="rest", bufs=3)
-            nc.vector.scalar_tensor_tensor(rest[:], whole[:], MAGIC, turns[:], ALU.subtract, ALU.subtract)
-            held["rest", i] = rest
-
-        def product(i):
-            sin = stage.tile([P, wide], F32, name="sin", bufs=3)
-            nc.scalar.activation(sin[:], held["rest", i][:], ACT.Sin, scale=-2.0 * math.pi)
-            b = first_stage("b", 3, i, wb_passes)
-            prod = stage.tile([P, wide], F32, name="prod", bufs=3)
-            nc.vector.tensor_tensor(prod[:], sin[:], b[:], ALU.mult)
-            held["prod", i] = prod
-
-        def donor_tanh(i):
-            d = first_stage("dy", 2, i, wd_passes)
-            tanh = keep.tile([P, wide], F32, name="tanh%d" % i)
-            nc.scalar.activation(tanh[:], d[:], ACT.Tanh)
-            held["tanh", i] = tanh
-
-        def larger(i):
-            jb, a, tp = steps[i]
-            tanh = held["tanh", i]
-            if tp == 0:
-                planar[jb, a] = stage.tile([P, 4, BLOCK], BF16, name="planar", bufs=3)
-            for s in range(2):
-                t = 2 * tp + s
-                c = slice(BLOCK * s, BLOCK * (s + 1))
-                nc.vector.scalar_tensor_tensor(
-                    planar[jb, a][:, t, :], tanh[:, c], gains[:, a, t : t + 1], held["prod", i][:, c], ALU.mult, ALU.max
-                )
-
-        def weave(jb, a, on_vector):
-            woven = stage.tile([P, 4 * BLOCK], BF16, name="woven", bufs=3, align_bytes=64)
-            dst = woven[:].rearrange("p (c i t) -> p c t i", i=4, t=4)
-            src = planar[jb, a][:].rearrange("p t (c i) -> p c t i", i=4)
-            if on_vector:
-                nc.vector.tensor_copy(dst, src)
-            else:
-                nc.scalar.copy(dst, src)
-            held["woven", jb, a] = woven
-
-        def quantise_h(jb, a):
-            codes = stage.tile([P, BLOCK], U32, name="h_codes", bufs=4, align_bytes=64)
-            plane = stage.tile([P, BLOCK], U8, name="h_plane", bufs=4, align_bytes=64)
-            nc.vector.quantize_mx(codes[:].bitcast(FP8X4), plane[:], held["woven", jb, a][:])
-            hq[jb, a] = (codes, plane)
-
-        def second_stage(jb, u):
-            y = psum.tile([P, BLOCK], F32, name="dy", bufs=2)
-            ucols = slice(P * u, P * (u + 1))
-            for a in range(2):
-                codes, plane = hq[jb, a]
-                nc.tensor.matmul_mx(
-                    y[:], lhsT=wo_codes[a][:, ucols].bitcast(FP8X4), lhsT_scale=wo_plane[4 * a :, ucols],
-                    rhs=codes[:].bitcast(FP8X4), rhs_scale=plane[:], start=(a == 0), stop=(a == 1),
-                )
-            y_sb = stage.tile([P, BLOCK], F32, name="y_sb", bufs=4)
-            nc.scalar.copy(y_sb[:], y[:])
-            lst = list3[:, BLOCK * jb // 16 : BLOCK * (jb + 1) // 16]
-            nc.vector.tensor_tensor(page[u][:].indirect(lst), y_sb[:], gate[:, BLOCK * jb : BLOCK * (jb + 1)], ALU.mult)
-            if jb == S // BLOCK - 1:
-                nc.sync.dma_start(out[P * u : P * (u + 1), :], page[u][:])
-
-        count = len(steps)
-        LAG = 1
         for a in range(2):
             for i in range(count):
                 if steps[i][1] == a:
                     donor_tanh(i)
-        v = {}
-        v[0, 0] = gather_words("v00", table[0], list1, 0)
-        w1q = {(0, 0): quantise_weight("w1_00", raw_w1[0, 0], 128)}
-        v[1, 0] = gather_words("v10", table[1], list1, 0)
-        w1q[1, 0] = quantise_weight("w1_10", raw_w1[1, 0], 128)
+        for kp in range(2):
+            v[kp, 0] = gather_words(kept_words("v%d_0" % kp), table[kp], list1, 0)
+            w1q[kp, 0] = quantise_weight("w1_%d0" % kp, raw_w1[kp, 0], nc.vector.tensor_copy)
         wb_codes = keep.tile([P, 2 * H], U8, name="wb_codes", align_bytes=64)
         nc.vector.tensor_copy(
-            wb_codes[:].bitcast(U16).rearrange("p (a t m) -> p a m t", a=2, t=4),
-            wb_raw[:].bitcast(U16).rearrange("p (a m t) -> p a m t", a=2, t=4),
+            wb_codes[:].bitcast(U16).rearrange("p (a t m) -> p a t m", a=2, t=4),
+            wb_raw[:].bitcast(U16).rearrange("p (a m t) -> p a t m", a=2, t=4),
         )
-        wb_plane = keep.tile([P, H], U8, name="wb_plane", align_bytes=64)
+        wb_scale_tile = keep.tile([P, H], U8, name="wb_scale_tile", align_bytes=64)
         nc.vector.tensor_copy(
-            wb_plane[:].rearrange("p (a t m) -> p a t m", a=2, t=4),
+            wb_scale_tile[:].rearrange("p (a t m) -> p a t m", a=2, t=4),
             wb_rows[:].rearrange("p (a m t) -> p a t m", a=2, t=4),
         )
-        for step in range(count + LAG + 9):
-            if step == 1:
-                w1q[0, 1] = quantise_weight("w1_01", raw_w1[0, 1], 0)
-            if step == 2:
-                w1q[1, 1] = quantise_weight("w1_11", raw_w1[1, 1], 64)
-            if step == 5:
-                v[0, 1] = gather_words("v01", table[0], list1, 1)
-            if step == 6:
-                v[1, 1] = gather_words("v11", table[1], list1, 1)
-            if step < count:
-                reduce_angle(step)
-            if 0 <= step - LAG < count:
-                product(step - LAG)
-            if 0 <= step - LAG - 1 < count:
-                larger(step - LAG - 1)
-            i = step - LAG - 2
-            if 0 <= i < count and i % 2 == 1:
-                weave(steps[i][0], steps[i][1], i == count - 1)
-            i = step - LAG - 3
-            if 0 <= i < count and i % 2 == 1:
-                quantise_h(steps[i][0], steps[i][1])
-            i = step - LAG - 7
-            if 0 <= i < count:
-                second_stage(i // 4, i % 4)
+
+        last = BLOCKS - 1
+        places = [(jb, u) for jb in range(BLOCKS) for u in range(PAGES) if (jb, u) != (last - 1, PAGES - 1)]
+        places = places[:-1] + [(last - 1, PAGES - 1)] + places[-1:]
+        filler = (last - 1, PAGES - 2)
+        first_place = 2 * EARLY_WEAVES + 1
+
+        for i in range(AHEAD):
+            count_turns(i)
+        for i in range(count):
+            if i < 2:
+                w1q[i, 1] = quantise_weight("w1_%d1" % i, raw_w1[i, 1], nc.vector.tensor_copy)
+            elif i < 4:
+                v[i - 2, 1] = gather_words(rounded_buffer([P, HALF], U32), table[i - 2], list1, 1)
+            sine_times_b(i)
+            if i % 2 == 1 and i > 1:
+                quantise_h(units[i // 2 - 1])
+            larger(i)
+            if i + AHEAD < count:
+                count_turns(i + AHEAD)
+            if i % 2 == 0 and i > 0:
+                done = i // 2 - 1
+                weave(units[done], nc.vector.tensor_copy if done < EARLY_WEAVES else nc.scalar.copy)
+            if first_place <= i < count - 1:
+                place(*places[i - first_place])
+        placed = count - 1 - first_place
+        for jb, u in places[placed : places.index(filler)]:
+            place(jb, u)
+        weave(units[-1], nc.vector.tensor_copy)
+        quantise_h(units[-1])
+        for jb, u in places[places.index(filler) :]:
+            place(jb, u)

import math
from contextlib import ExitStack

import concourse.mybir as mybir
from concourse.masks import make_identity

T, S, K, M, H, N = 2048, 1024, 1024, 512, 1024, 512
FLOPS = 2 * S * (K * H + 2 * M * H + H * N)

F32 = mybir.dt.float32
BF16 = mybir.dt.bfloat16
I32 = mybir.dt.int32
U32 = mybir.dt.uint32
U16 = mybir.dt.uint16
U8 = mybir.dt.uint8
FP8X4 = mybir.dt.float8_e4m3fn_x4
FP4X4 = mybir.dt.float4_e2m1fn_x4
ALU = mybir.AluOpType
ACT = mybir.ActivationFunctionType

P = 128
PASS = 512
HALF = S // 2
BLOCK = 256
BLOCKS = S // BLOCK
PAGES = N // P

OFFSET = 1.5 * 2.0**16
OFFSET_BITS = float(0x47C00000)

AHEAD = 3
TURN_BUFS = AHEAD + 2
EARLY_WEAVES = 3


def tile_list_scratch_repair_ranker_kernel(
    tc, tab_words, tab_scales, tab2_words, tab2_scales, offs, offs2, offs3,
    w1, wb_words, wb_scales, wd, gd, wo_words, wo_scales, page1, wgo, out,
):
    nc = tc.nc
    with ExitStack() as ctx:
        keep = ctx.enter_context(tc.tile_pool(name="keep", bufs=1))
        stage = ctx.enter_context(tc.tile_pool(name="stage", bufs=3))
        psum = ctx.enter_context(tc.psum_pool(name="psum", bufs=2))

        def zeroed_scale_tile(name, width):
            tile = keep.tile([P, width], U8, name=name, align_bytes=64)
            nc.vector.memset(tile[:].bitcast(I32), 0)
            return tile

        def load_list(name, src):
            tile = keep.tile([P, S // 16], U16, name=name)
            nc.sync.dma_start(tile[:], src)
            return tile

        def load_words(name, src):
            tile = keep.tile([P, src.shape[1]], I32, name=name, align_bytes=64)
            nc.sync.dma_start(tile[:], src.rearrange("p c i -> p (c i)").bitcast(I32))
            return tile

        def load_scale_rows(tile, src):
            for d in range(4):
                nc.sync.dma_start(tile[32 * d : 32 * d + 4, :].bitcast(I32), src[4 * d : 4 * d + 4, :].bitcast(I32))

        def load_weight(src, kp, a):
            raw = stage.tile([P, 4, PASS], F32, name="raw", bufs=4, align_bytes=64)
            rows = src[PASS * kp : PASS * (kp + 1), PASS * a : PASS * (a + 1)]
            nc.sync.dma_start(raw[:], rows.rearrange("(p j) c -> p j c", j=4))
            return raw

        def rounded_buffer(shape, dtype):
            return stage.tile(shape, dtype, name="rounded", bufs=2, align_bytes=64)

        def quantise_weight(name, raw, cast):
            rounded = rounded_buffer([P, 4 * PASS], BF16)
            cast(
                rounded[:].rearrange("p (h e m j) -> p h m j e", h=2, e=2, j=4),
                raw[:].rearrange("p j (m h e) -> p h m j e", h=2, e=2),
            )
            codes = keep.tile([P, PASS], U32, name=name + "_codes", align_bytes=64)
            scales = keep.tile([P, PASS], U8, name=name + "_scales", align_bytes=64)
            nc.vector.quantize_mx(codes[:].bitcast(FP8X4), scales[:], rounded[:])
            return codes, scales

        def gather_words(picked, table, offsets, half):
            cols = slice(half * HALF // 16, (half + 1) * HALF // 16)
            nc.vector.tensor_copy(picked[:], table[:].bitcast(U32).indirect(offsets[:, cols]))
            return picked

        def kept_words(name):
            return keep.tile([P, HALF], U32, name=name, align_bytes=64)

        units = [(0, 0), (1, 0), (0, 1), (1, 1)] + [(jb, a) for jb in range(2, BLOCKS) for a in range(2)]
        steps = [(jb, a, part) for jb, a in units for part in range(2)]
        count = len(steps)
        wide = 2 * BLOCK
        table, v, v2, w1q, wdq = {}, {}, {}, {}, {}
        tanh, turns, offset_less_whole, prod, planes, woven, hq = {}, {}, {}, {}, {}, {}, {}

        def donor_product(bank_name, i, weight_columns):
            jb, a, part = steps[i]
            half, c0 = divmod(BLOCK * jb, HALF)
            bank = psum.tile([P, wide], F32, name=bank_name)
            for s in range(2):
                codes, scales = weight_columns(a, 2 * part + s)
                nc.tensor.matmul_mx(
                    bank[:, BLOCK * s : BLOCK * (s + 1)], lhsT=codes, lhsT_scale=scales,
                    rhs=v2[half][:, c0 : c0 + BLOCK].bitcast(FP8X4),
                    rhs_scale=v2_scales[:, BLOCK * jb : BLOCK * (jb + 1)], start=True, stop=True,
                )
            return bank

        def wd_columns(a, t):
            c = slice(P * t, P * (t + 1))
            return wdq[a][0][:, c].bitcast(FP8X4), wdq[a][1][:, c]

        def wb_columns(a, t):
            c0 = PASS * a + P * t
            return wb_codes[:, 2 * c0 : 2 * (c0 + P)].bitcast(FP4X4), wb_scale_tile[:, c0 : c0 + P]

        def donor_tanh(i):
            d = donor_product(("y", "b")[i % 2], i, wd_columns)
            tanh[i] = keep.tile([P, wide], F32, name="tanh%d" % i)
            nc.scalar.activation(tanh[i][:], d[:], ACT.Tanh)

        def count_turns(i):
            jb, a, part = steps[i]
            j0 = BLOCK * jb + P * part
            half, c0 = divmod(j0, HALF)
            f = psum.tile([P, PASS], F32, name="f")
            for kp in range(2):
                nc.tensor.matmul_mx(
                    f[:], lhsT=v[kp, half][:, c0 : c0 + P].bitcast(FP8X4), lhsT_scale=v_scales[4 * kp :, j0 : j0 + P],
                    rhs=w1q[kp, a][0][:].bitcast(FP8X4), rhs_scale=w1q[kp, a][1][:], start=(kp == 0), stop=(kp == 1),
                )
            turns[i] = stage.tile([P, PASS], F32, name="turns", bufs=TURN_BUFS)
            nc.scalar.activation(turns[i][:], f[:], ACT.Copy, bias=0.0, scale=1.0 / (2.0 * math.pi))
            offset_less_whole[i] = stage.tile([P, PASS], U32, name="offset_less_whole", bufs=TURN_BUFS)
            nc.scalar.activation(offset_less_whole[i][:], f[:], ACT.Copy, bias=OFFSET_BITS, scale=-128.0 / (2.0 * math.pi))

        def sine_times_b(i):
            jb, a, part = steps[i]
            rest = psum.tile([P, wide], F32, name="rest")
            for s in range(2):
                c = slice(P * (2 * part + s), P * (2 * part + s + 1))
                for entries in range(2):
                    source = i - part + entries
                    terms = [offset_less_whole[source][:].bitcast(F32)[:, c], minus_offset[:], turns[source][:, c]]
                    for n, term in enumerate(terms):
                        nc.tensor.matmul(
                            rest[:, BLOCK * s + P * entries : BLOCK * s + P * (entries + 1)], lhsT=term, rhs=ident[:],
                            is_transpose=True, start=(n == 0), stop=(n == len(terms) - 1),
                        )
            sine = stage.tile([P, wide], F32, name="sine", bufs=4)
            nc.scalar.activation(sine[:], rest[:], ACT.Sin, scale=2.0 * math.pi)
            b = donor_product("b", i, wb_columns)
            prod[i] = stage.tile([P, wide], F32, name="prod")
            for s in range(2):
                c = slice(BLOCK * s, BLOCK * (s + 1))
                nc.vector.tensor_tensor(prod[i][:, c], sine[:, c], b[:, c], ALU.mult)

        def larger(i):
            jb, a, part = steps[i]
            if (jb, a, part) == (*units[-1], 0):
                planes[jb, a] = stage.tile([P, 4, BLOCK], BF16, name="last_planes", bufs=1)
            elif part == 0:
                planes[jb, a] = stage.tile([P, 4, BLOCK], BF16, name="planes")
            for s in range(2):
                t = 2 * part + s
                c = slice(BLOCK * s, BLOCK * (s + 1))
                nc.vector.scalar_tensor_tensor(
                    planes[jb, a][:, t, :], tanh[i][:, c], gains[:, a, t : t + 1], prod[i][:, c], ALU.mult, ALU.max
                )

        def weave(unit, copy):
            woven[unit] = stage.tile([P, 4 * BLOCK], BF16, name="woven", align_bytes=64)
            copy(
                woven[unit][:].rearrange("p (c i t) -> p c t i", i=4, t=4),
                planes[unit][:].rearrange("p t (c i) -> p c t i", i=4),
            )

        def quantise_h(unit):
            codes = stage.tile([P, BLOCK], U32, name="h_codes", bufs=5, align_bytes=64)
            scales = stage.tile([P, BLOCK], U8, name="h_scales", bufs=5, align_bytes=64)
            nc.vector.quantize_mx(codes[:].bitcast(FP8X4), scales[:], woven[unit][:])
            hq[unit] = (codes, scales)

        def place(jb, u):
            y = psum.tile([P, BLOCK], F32, name="y")
            c = slice(P * u, P * (u + 1))
            for a in range(2):
                codes, scales = hq[jb, a]
                nc.tensor.matmul_mx(
                    y[:], lhsT=wo_codes[a][:, c].bitcast(FP8X4), lhsT_scale=wo_scale_tile[4 * a :, c],
                    rhs=codes[:].bitcast(FP8X4), rhs_scale=scales[:], start=(a == 0), stop=(a == 1),
                )
            if (jb, u) == filler:
                y_sb = stage.tile([P, BLOCK], F32, name="last_planes", bufs=1)
            else:
                y_sb = stage.tile([P, BLOCK], F32, name="y_sb", bufs=PAGES)
            nc.scalar.copy(y_sb[:], y[:])
            offsets = list3[:, BLOCK * jb // 16 : BLOCK * (jb + 1) // 16]
            nc.vector.tensor_tensor(page[u][:].indirect(offsets), y_sb[:], gate[:, BLOCK * jb : BLOCK * (jb + 1)], ALU.mult)
            if jb == BLOCKS - 1:
                nc.sync.dma_start(out[P * u : P * (u + 1), :], page[u][:])

        ident = keep.tile([P, P], F32, name="ident")
        make_identity(nc, ident[:])
        minus_offset = keep.tile([P, P], F32, name="minus_offset")
        nc.gpsimd.memset(minus_offset[:], -OFFSET)
        tab2_rows = zeroed_scale_tile("tab2_rows", T)
        tab_rows = zeroed_scale_tile("tab_rows", T)
        wb_rows = zeroed_scale_tile("wb_rows", H)
        wo_scale_tile = zeroed_scale_tile("wo_scale_tile", N)

        list1 = load_list("list1", offs)
        list2 = load_list("list2", offs2)
        list3 = load_list("list3", offs3)
        gains = keep.tile([P, 2, 4], F32, name="gains")
        nc.sync.dma_start(gains[:], gd.rearrange("(a p t) -> p a t", a=2, t=4))
        table2 = load_words("table2", tab2_words[0])
        wb_raw = keep.tile([P, 2 * H], U8, name="wb_raw")
        nc.sync.dma_start(wb_raw[:].bitcast(I32), wb_words[0].bitcast(I32))
        load_scale_rows(tab2_rows, tab2_scales[0])
        raw_wd = [load_weight(wd, 0, 0)]
        for kp in range(2):
            for odd in range(2):
                src = tab_scales[kp].rearrange("(g odd) t -> odd g t", odd=2)[odd]
                nc.sync.dma_start(tab_rows[4 * kp + odd : P : 16, :].bitcast(I32), src.bitcast(I32))
        raw_wd.append(load_weight(wd, 0, 1))
        table[0] = load_words("table0", tab_words[0])
        raw_w1 = {(0, 0): load_weight(w1, 0, 0)}
        table[1] = load_words("table1", tab_words[1])

        v2[0] = gather_words(kept_words("v2_0"), table2, list2, 0)
        v2_scales = keep.tile([P, S], U8, name="v2_scales", align_bytes=64)
        nc.vector.tensor_copy(v2_scales[:], tab2_rows[:].indirect(list2[:]))
        v2[1] = gather_words(kept_words("v2_1"), table2, list2, 1)
        wdq[0] = quantise_weight("wd_0", raw_wd[0], nc.scalar.copy)
        v_rows = keep.tile([P, S], U8, name="v_rows", align_bytes=64)
        nc.vector.tensor_copy(v_rows[:], tab_rows[:].indirect(list1[:]))
        v_scales = keep.tile([P, S], U8, name="v_scales", align_bytes=64)
        nc.vector.tensor_copy(v_scales[:].bitcast(I32), v_rows[:].bitcast(I32))
        wdq[1] = quantise_weight("wd_1", raw_wd[1], nc.scalar.copy)
        raw_w1[1, 0] = load_weight(w1, 1, 0)
        for kp in range(2):
            for odd in range(2):
                nc.sync.dma_start(
                    v_scales[4 * kp + 2 + odd : P : 32, :].bitcast(I32),
                    v_rows[16 + 4 * kp + odd : P : 32, :].bitcast(I32),
                )
        raw_w1[0, 1] = load_weight(w1, 0, 1)
        raw_w1[1, 1] = load_weight(w1, 1, 1)
        load_scale_rows(wb_rows, wb_scales[0])
        wo_codes = [load_words("wo%d" % a, wo_words[a]) for a in range(2)]
        for d in range(4):
            nc.sync.dma_start(
                wo_scale_tile[32 * d : 32 * d + 8, :].bitcast(I32), wo_scales[:, 4 * d : 4 * d + 4, :].bitcast(I32)
            )
        gate = keep.tile([P, S], F32, name="gate")
        nc.sync.dma_start(gate[:], wgo)
        page = []
        for u in range(PAGES):
            page.append(keep.tile([P, T], F32, name="page%d" % u))
            nc.sync.dma_start(page[u][:], page1[P * u : P * (u + 1), :])

        for a in range(2):
            for i in range(count):
                if steps[i][1] == a:
                    donor_tanh(i)
        for kp in range(2):
            v[kp, 0] = gather_words(kept_words("v%d_0" % kp), table[kp], list1, 0)
            w1q[kp, 0] = quantise_weight("w1_%d0" % kp, raw_w1[kp, 0], nc.vector.tensor_copy)
        wb_codes = keep.tile([P, 2 * H], U8, name="wb_codes", align_bytes=64)
        nc.vector.tensor_copy(
            wb_codes[:].bitcast(U16).rearrange("p (a t m) -> p a t m", a=2, t=4),
            wb_raw[:].bitcast(U16).rearrange("p (a m t) -> p a t m", a=2, t=4),
        )
        wb_scale_tile = keep.tile([P, H], U8, name="wb_scale_tile", align_bytes=64)
        nc.vector.tensor_copy(
            wb_scale_tile[:].rearrange("p (a t m) -> p a t m", a=2, t=4),
            wb_rows[:].rearrange("p (a m t) -> p a t m", a=2, t=4),
        )

        last = BLOCKS - 1
        places = [(jb, u) for jb in range(BLOCKS) for u in range(PAGES) if (jb, u) != (last - 1, PAGES - 1)]
        places = places[:-1] + [(last - 1, PAGES - 1)] + places[-1:]
        filler = (last - 1, PAGES - 2)
        first_place = 2 * EARLY_WEAVES + 1

        for i in range(AHEAD):
            count_turns(i)
        for i in range(count):
            if i < 2:
                w1q[i, 1] = quantise_weight("w1_%d1" % i, raw_w1[i, 1], nc.vector.tensor_copy)
            elif i < 4:
                v[i - 2, 1] = gather_words(rounded_buffer([P, HALF], U32), table[i - 2], list1, 1)
            sine_times_b(i)
            if i % 2 == 1 and i > 1:
                quantise_h(units[i // 2 - 1])
            larger(i)
            if i + AHEAD < count:
                count_turns(i + AHEAD)
            if i % 2 == 0 and i > 0:
                done = i // 2 - 1
                weave(units[done], nc.vector.tensor_copy if done < EARLY_WEAVES else nc.scalar.copy)
            if first_place <= i < count - 1:
                place(*places[i - first_place])
        placed = count - 1 - first_place
        for jb, u in places[placed : places.index(filler)]:
            place(jb, u)
        weave(units[-1], nc.vector.tensor_copy)
        quantise_h(units[-1])
        for jb, u in places[places.index(filler) :]:
            place(jb, u)
